import numpy as np
CORES = [388,396,404,412,420,428,436,444,452,460,468,476,484,492,500,508,124,252,380]
N = 19
def setup_inputs(rng):
    return {"x": rng.standard_normal((N, 128, 1024), dtype=np.float32)}
def reference(x):
    s = np.cumsum(x.astype(np.float64), axis=0)
    y = np.full(x.shape, np.nan, x.dtype)
    y[1:] = s[:-1]
    return {"y": y}

@@ -1,0 +1,115 @@
+from concourse.bass import DstId, RemoteDMATransfer
+
+NS, W = 64, 16
+SCRATCH = {
+    "a": ("dram", [NS, 128, W], "float32"),
+    "b": ("dram", [NS, 128, W], "float32"),
+    "o": ("dram", [17, 128, W], "float32"),
+}
+SEMAPHORES = ["ld0", "ld1", "ld2", "ld3",
+              "hin",
+              "xin",
+              "tin",
+              "res0", "res1", "res2", "res3",
+              "sent",
+              "st0", "st1"]
+
+PORT = ((6, 7), (2, 3))
+PLAIN = ((4, 5), (0, 1))
+
+
+def _group(gi):
+    return gi // 4, (gi // 2) % 2, gi % 2
+
+
+def _home(t, host):
+    d, par, q = _group(t // 8)
+    return host * 128 + (2 * (t % 8) + par) * 8 + PORT[d][q]
+
+
+def _sender(gi, parity):
+    d, par, q = _group(gi)
+    return (PLAIN if par == parity else PORT)[d][q]
+
+
+def rank_program(g, core, T, topo):
+    host, chip, k = topo.host(core), topo.chip(core), core % 8
+    base = core - k
+    rank = T.rank_of(core)
+    chip_rank = T.rank_of(base + 4)
+    sem = T.sem
+    sent = [0]
+
+    def xfer(dst, out, srcs, engines, rsem):
+        rid, pid = topo.addr(dst, core)
+        n = 0
+        for e in range(16):
+            n += (engines >> e) & 1
+        sent[0] += n
+        if len(srcs) == 1:
+            return RemoteDMATransfer(dst_ids=[DstId(rid=rid, pnc=pid)], dma_engine_mask=engines, remote_sem=rsem,
+                                     src=srcs[0], dst=out, alu_op=0)
+        return RemoteDMATransfer(dst_ids=[DstId(rid=rid, pnc=pid)], dma_engine_mask=engines, remote_sem=rsem,
+                                 srcs=srcs, dsts=[out], alu_op=1)
+
+    def scatter(t, engine):
+        to_host, slot = (2, chip_rank) if chip_rank < 16 else (1, chip_rank - 16)
+        return xfer(_home(t, to_host), T.o[slot], [T.a[t]], 1 << engine, sem.xin)
+
+    if rank is not None and rank < 18:
+        for p in range(4):
+            q = g.sync if p % 2 == 0 else g.scalar
+            q.dma_start(T.a[16 * p:16 * p + 16], T.x[32 * p:32 * p + 32, :]).then_inc(sem["ld%d" % p], 16)
+        for p in range(4):
+            g.wait_ge(sem["ld%d" % p], 16)
+            tr = []
+            for i in range(16):
+                t = 16 * p + i
+                s = _sender(t // 8, chip % 2)
+                if s == k:
+                    tr.append(scatter(t, i))
+                else:
+                    tr.append(xfer(base + s, T.a[t], [T.a[t]], 1 << i, sem.hin))
+            g.remote_dma_fused(tr, local_sem=sem.sent)
+
+    if rank is None and chip_rank is not None and chip_rank < 18:
+        gi = [j for j in range(8) if _sender(j, chip % 2) == k][0]
+        g.wait_ge(sem.hin, 8)
+        g.remote_dma_fused([scatter(8 * gi + m, m) for m in range(8)], local_sem=sem.sent)
+
+    mine = [t for t in range(NS) if _home(t, host) == core]
+
+    if host == 2 and mine:
+        t = mine[0]
+        res = sem["res%d" % (t // 16)]
+
+        def prefix(r, engines):
+            return xfer(T.cores[r], T.b[t], [T.o[j] for j in range(min(r, 17))], engines, res)
+
+        g.wait_ge(sem.xin, 16)
+        g.remote_dma_fused([xfer(_home(t, 1), T.o[2], [T.o[j] for j in range(16)], 0xFF, sem.tin)], local_sem=sem.sent)
+        g.remote_dma_fused([prefix(15 - e, 1 << e) for e in range(7)] + [prefix(1, 1 << 7)], local_sem=sem.sent)
+        g.remote_dma_fused([prefix(2 + e, 1 << e) for e in range(7)], local_sem=sem.sent)
+        g.wait_ge(sem.tin, 8)
+        g.remote_dma_fused([prefix(18, 1 << 7)], local_sem=sem.sent)
+
+    if host == 1 and mine:
+        t = mine[0]
+        res = sem["res%d" % (t // 16)]
+        g.wait_ge(sem.xin, 2)
+        g.remote_dma_fused([xfer(_home(t, 2), T.o[16], [T.o[0], T.o[1]], 0xFF, sem.tin)], local_sem=sem.sent)
+        g.wait_ge(sem.tin, 8)
+        g.remote_dma_fused([xfer(T.cores[16], T.b[t], [T.o[2]], 0x0F, res),
+                            xfer(T.cores[17], T.b[t], [T.o[2], T.o[0]], 0xF0, res)], local_sem=sem.sent)
+
+    if rank is not None and rank > 0:
+        per = 4 if rank in (16, 17) else 1
+        for p in range(4):
+            q = g.sync if p % 2 == 0 else g.scalar
+            q.wait_ge(sem["res%d" % p], 16 * per)
+            q.dma_start(T.y[32 * p:32 * p + 32, :], T.b[16 * p:16 * p + 16]).then_inc(sem["st%d" % (p % 2)], 16)
+        g.wait_ge(sem.st0, 32)
+        g.wait_ge(sem.st1, 32)
+
+    if sent[0]:
+        g.wait_ge(sem.sent, sent[0])

@@ -1,10 +1,8 @@
 from concourse.bass import DstId, RemoteDMATransfer
 
-NS, W = 64, 16
 SCRATCH = {
-    "a": ("dram", [NS, 128, W], "float32"),
-    "b": ("dram", [NS, 128, W], "float32"),
-    "o": ("dram", [17, 128, W], "float32"),
+    "ae": ("dram", [32, 128, 18], "float32"),
+    "ao": ("dram", [28, 128, 16], "float32"),
 }
 SEMAPHORES = ["ld0", "ld1", "ld2", "ld3",
               "hin",
@@ -16,20 +14,16 @@ SEMAPHORES = ["ld0", "ld1", "ld2", "ld3",
 
 PORT = ((6, 7), (2, 3))
 PLAIN = ((4, 5), (0, 1))
+PIECES = ((0, 0, 16, 0, 36), (0, 16, 16, 36, 36), (1, 0, 14, 72, 28), (1, 14, 14, 100, 28))
 
 
-def _group(gi):
-    return gi // 4, (gi // 2) % 2, gi % 2
+def _home(par, i, host):
+    n = 8 - par
+    return host * 128 + (2 * (i % n) + par) * 8 + PORT[i // n // 2][i // n % 2]
 
 
-def _home(t, host):
-    d, par, q = _group(t // 8)
-    return host * 128 + (2 * (t % 8) + par) * 8 + PORT[d][q]
-
-
-def _sender(gi, parity):
-    d, par, q = _group(gi)
-    return (PLAIN if par == parity else PORT)[d][q]
+def _sender(par, grp, parity):
+    return (PLAIN if par == parity else PORT)[grp // 2][grp % 2]
 
 
 def rank_program(g, core, T, topo):
@@ -38,76 +32,77 @@ def rank_program(g, core, T, topo):
     rank = T.rank_of(core)
     chip_rank = T.rank_of(base + 4)
     sem = T.sem
+    buf = (T.ae, T.ao)
     sent = [0]
 
     def xfer(dst, out, srcs, engines, rsem):
         rid, pid = topo.addr(dst, core)
-        n = 0
-        for e in range(16):
-            n += (engines >> e) & 1
-        sent[0] += n
+        sent[0] += sum((engines >> e) & 1 for e in range(16))
         if len(srcs) == 1:
             return RemoteDMATransfer(dst_ids=[DstId(rid=rid, pnc=pid)], dma_engine_mask=engines, remote_sem=rsem,
                                      src=srcs[0], dst=out, alu_op=0)
         return RemoteDMATransfer(dst_ids=[DstId(rid=rid, pnc=pid)], dma_engine_mask=engines, remote_sem=rsem,
                                  srcs=srcs, dsts=[out], alu_op=1)
 
-    def scatter(t, engine):
+    def scatter(par, i, engine):
         to_host, slot = (2, chip_rank) if chip_rank < 16 else (1, chip_rank - 16)
-        return xfer(_home(t, to_host), T.o[slot], [T.a[t]], 1 << engine, sem.xin)
+        return xfer(_home(par, i, to_host), buf[par][slot], [buf[par][i]], 1 << engine, sem.xin)
 
     if rank is not None and rank < 18:
-        for p in range(4):
+        for p, (par, s0, ns, r0, nr) in enumerate(PIECES):
             q = g.sync if p % 2 == 0 else g.scalar
-            q.dma_start(T.a[16 * p:16 * p + 16], T.x[32 * p:32 * p + 32, :]).then_inc(sem["ld%d" % p], 16)
-        for p in range(4):
+            q.dma_start(buf[par][s0:s0 + ns], T.x[r0:r0 + nr, :]).then_inc(sem["ld%d" % p], 16)
+        for p, (par, s0, ns, r0, nr) in enumerate(PIECES):
             g.wait_ge(sem["ld%d" % p], 16)
             tr = []
-            for i in range(16):
-                t = 16 * p + i
-                s = _sender(t // 8, chip % 2)
+            for e in range(ns):
+                i = s0 + e
+                s = _sender(par, i // (8 - par), chip % 2)
                 if s == k:
-                    tr.append(scatter(t, i))
+                    tr.append(scatter(par, i, e))
                 else:
-                    tr.append(xfer(base + s, T.a[t], [T.a[t]], 1 << i, sem.hin))
+                    tr.append(xfer(base + s, buf[par][i], [buf[par][i]], 1 << e, sem.hin))
             g.remote_dma_fused(tr, local_sem=sem.sent)
 
     if rank is None and chip_rank is not None and chip_rank < 18:
-        gi = [j for j in range(8) if _sender(j, chip % 2) == k][0]
-        g.wait_ge(sem.hin, 8)
-        g.remote_dma_fused([scatter(8 * gi + m, m) for m in range(8)], local_sem=sem.sent)
+        par, grp = [(a, b) for a in range(2) for b in range(4) if _sender(a, b, chip % 2) == k][0]
+        n = 8 - par
+        g.wait_ge(sem.hin, n)
+        g.remote_dma_fused([scatter(par, grp * n + m, m) for m in range(n)], local_sem=sem.sent)
 
-    mine = [t for t in range(NS) if _home(t, host) == core]
+    mine = [(a, i) for a in range(2) for i in range(4 * (8 - a)) if _home(a, i, host) == core]
 
     if host == 2 and mine:
-        t = mine[0]
-        res = sem["res%d" % (t // 16)]
+        par, i = mine[0]
+        o = buf[par]
+        res = sem["res%d" % (2 * par + i // (16 - 2 * par))]
 
         def prefix(r, engines):
-            return xfer(T.cores[r], T.b[t], [T.o[j] for j in range(min(r, 17))], engines, res)
+            return xfer(T.cores[r], o[i], [o[j] for j in range(min(r, 17))], engines, res)
 
         g.wait_ge(sem.xin, 16)
-        g.remote_dma_fused([xfer(_home(t, 1), T.o[2], [T.o[j] for j in range(16)], 0xFF, sem.tin)], local_sem=sem.sent)
+        g.remote_dma_fused([xfer(_home(par, i, 1), o[2], [o[j] for j in range(16)], 0xFF, sem.tin)], local_sem=sem.sent)
         g.remote_dma_fused([prefix(15 - e, 1 << e) for e in range(7)] + [prefix(1, 1 << 7)], local_sem=sem.sent)
         g.remote_dma_fused([prefix(2 + e, 1 << e) for e in range(7)], local_sem=sem.sent)
         g.wait_ge(sem.tin, 8)
         g.remote_dma_fused([prefix(18, 1 << 7)], local_sem=sem.sent)
 
     if host == 1 and mine:
-        t = mine[0]
-        res = sem["res%d" % (t // 16)]
+        par, i = mine[0]
+        o = buf[par]
+        res = sem["res%d" % (2 * par + i // (16 - 2 * par))]
         g.wait_ge(sem.xin, 2)
-        g.remote_dma_fused([xfer(_home(t, 2), T.o[16], [T.o[0], T.o[1]], 0xFF, sem.tin)], local_sem=sem.sent)
+        g.remote_dma_fused([xfer(_home(par, i, 2), o[16], [o[0], o[1]], 0xFF, sem.tin)], local_sem=sem.sent)
         g.wait_ge(sem.tin, 8)
-        g.remote_dma_fused([xfer(T.cores[16], T.b[t], [T.o[2]], 0x0F, res),
-                            xfer(T.cores[17], T.b[t], [T.o[2], T.o[0]], 0xF0, res)], local_sem=sem.sent)
+        g.remote_dma_fused([xfer(T.cores[16], o[i], [o[2]], 0x0F, res),
+                            xfer(T.cores[17], o[i], [o[2], o[0]], 0xF0, res)], local_sem=sem.sent)
 
     if rank is not None and rank > 0:
         per = 4 if rank in (16, 17) else 1
-        for p in range(4):
+        for p, (par, s0, ns, r0, nr) in enumerate(PIECES):
             q = g.sync if p % 2 == 0 else g.scalar
-            q.wait_ge(sem["res%d" % p], 16 * per)
-            q.dma_start(T.y[32 * p:32 * p + 32, :], T.b[16 * p:16 * p + 16]).then_inc(sem["st%d" % (p % 2)], 16)
+            q.wait_ge(sem["res%d" % p], ns * per)
+            q.dma_start(T.y[r0:r0 + nr, :], buf[par][s0:s0 + ns]).then_inc(sem["st%d" % (p % 2)], 16)
         g.wait_ge(sem.st0, 32)
         g.wait_ge(sem.st1, 32)
 

from concourse.bass import DstId, RemoteDMATransfer

SCRATCH = {
    "ae": ("dram", [32, 128, 18], "float32"),
    "ao": ("dram", [28, 128, 16], "float32"),
}
SEMAPHORES = ["ld0", "ld1", "ld2", "ld3",
              "hin",
              "xin",
              "tin",
              "res0", "res1", "res2", "res3",
              "sent",
              "st0", "st1"]

PORT = ((6, 7), (2, 3))
PLAIN = ((4, 5), (0, 1))
PIECES = ((0, 0, 16, 0, 36), (0, 16, 16, 36, 36), (1, 0, 14, 72, 28), (1, 14, 14, 100, 28))


def _home(par, i, host):
    n = 8 - par
    return host * 128 + (2 * (i % n) + par) * 8 + PORT[i // n // 2][i // n % 2]


def _sender(par, grp, parity):
    return (PLAIN if par == parity else PORT)[grp // 2][grp % 2]


def rank_program(g, core, T, topo):
    host, chip, k = topo.host(core), topo.chip(core), core % 8
    base = core - k
    rank = T.rank_of(core)
    chip_rank = T.rank_of(base + 4)
    sem = T.sem
    buf = (T.ae, T.ao)
    sent = [0]

    def xfer(dst, out, srcs, engines, rsem):
        rid, pid = topo.addr(dst, core)
        sent[0] += sum((engines >> e) & 1 for e in range(16))
        if len(srcs) == 1:
            return RemoteDMATransfer(dst_ids=[DstId(rid=rid, pnc=pid)], dma_engine_mask=engines, remote_sem=rsem,
                                     src=srcs[0], dst=out, alu_op=0)
        return RemoteDMATransfer(dst_ids=[DstId(rid=rid, pnc=pid)], dma_engine_mask=engines, remote_sem=rsem,
                                 srcs=srcs, dsts=[out], alu_op=1)

    def scatter(par, i, engine):
        to_host, slot = (2, chip_rank) if chip_rank < 16 else (1, chip_rank - 16)
        return xfer(_home(par, i, to_host), buf[par][slot], [buf[par][i]], 1 << engine, sem.xin)

    if rank is not None and rank < 18:
        for p, (par, s0, ns, r0, nr) in enumerate(PIECES):
            q = g.sync if p % 2 == 0 else g.scalar
            q.dma_start(buf[par][s0:s0 + ns], T.x[r0:r0 + nr, :]).then_inc(sem["ld%d" % p], 16)
        for p, (par, s0, ns, r0, nr) in enumerate(PIECES):
            g.wait_ge(sem["ld%d" % p], 16)
            tr = []
            for e in range(ns):
                i = s0 + e
                s = _sender(par, i // (8 - par), chip % 2)
                if s == k:
                    tr.append(scatter(par, i, e))
                else:
                    tr.append(xfer(base + s, buf[par][i], [buf[par][i]], 1 << e, sem.hin))
            g.remote_dma_fused(tr, local_sem=sem.sent)

    if rank is None and chip_rank is not None and chip_rank < 18:
        par, grp = [(a, b) for a in range(2) for b in range(4) if _sender(a, b, chip % 2) == k][0]
        n = 8 - par
        g.wait_ge(sem.hin, n)
        g.remote_dma_fused([scatter(par, grp * n + m, m) for m in range(n)], local_sem=sem.sent)

    mine = [(a, i) for a in range(2) for i in range(4 * (8 - a)) if _home(a, i, host) == core]

    if host == 2 and mine:
        par, i = mine[0]
        o = buf[par]
        res = sem["res%d" % (2 * par + i // (16 - 2 * par))]

        def prefix(r, engines):
            return xfer(T.cores[r], o[i], [o[j] for j in range(min(r, 17))], engines, res)

        g.wait_ge(sem.xin, 16)
        g.remote_dma_fused([xfer(_home(par, i, 1), o[2], [o[j] for j in range(16)], 0xFF, sem.tin)], local_sem=sem.sent)
        g.remote_dma_fused([prefix(15 - e, 1 << e) for e in range(7)] + [prefix(1, 1 << 7)], local_sem=sem.sent)
        g.remote_dma_fused([prefix(2 + e, 1 << e) for e in range(7)], local_sem=sem.sent)
        g.wait_ge(sem.tin, 8)
        g.remote_dma_fused([prefix(18, 1 << 7)], local_sem=sem.sent)

    if host == 1 and mine:
        par, i = mine[0]
        o = buf[par]
        res = sem["res%d" % (2 * par + i // (16 - 2 * par))]
        g.wait_ge(sem.xin, 2)
        g.remote_dma_fused([xfer(_home(par, i, 2), o[16], [o[0], o[1]], 0xFF, sem.tin)], local_sem=sem.sent)
        g.wait_ge(sem.tin, 8)
        g.remote_dma_fused([xfer(T.cores[16], o[i], [o[2]], 0x0F, res),
                            xfer(T.cores[17], o[i], [o[2], o[0]], 0xF0, res)], local_sem=sem.sent)

    if rank is not None and rank > 0:
        per = 4 if rank in (16, 17) else 1
        for p, (par, s0, ns, r0, nr) in enumerate(PIECES):
            q = g.sync if p % 2 == 0 else g.scalar
            q.wait_ge(sem["res%d" % p], ns * per)
            q.dma_start(T.y[r0:r0 + nr, :], buf[par][s0:s0 + ns]).then_inc(sem["st%d" % (p % 2)], 16)
        g.wait_ge(sem.st0, 32)
        g.wait_ge(sem.st1, 32)

    if sent[0]:
        g.wait_ge(sem.sent, sent[0])
